import numpy as np
import ml_dtypes


def mxq(x, axis, fmt="e4m3"):
    dtype, down = {"e4m3": (ml_dtypes.float8_e4m3fn, 7), "e5m2": (ml_dtypes.float8_e5m2, 14)}[fmt]
    v = np.moveaxis(np.asarray(x, np.float32).astype(ml_dtypes.bfloat16).astype(np.float64), axis, -1)
    blocks = v.reshape(v.shape[:-1] + (-1, 32))
    amax = np.abs(blocks).max(-1, keepdims=True)
    byte = np.maximum(np.where(amax > 0, np.frexp(amax)[1] - 1 + 127, 0) - down, 1)
    scale = np.exp2(byte - 127.0)
    codes = (blocks / scale).astype(np.float32).astype(dtype).astype(np.float64)
    return np.moveaxis((codes * scale).reshape(v.shape), -1, axis)


WIDE = False


def mx_kscale(k):
    if not WIDE:
        return np.ones(k)
    levels = np.array([10, -10, 5, -5, 0])
    if k % 512:
        return np.exp2(np.random.permutation(np.resize(levels, k // 32))).repeat(32)
    a = np.empty((k // 512, 16))
    for p in range(k // 512):
        a[p, :8] = np.random.permutation(np.resize(levels, 8))
        for g in range(8):
            far = levels[np.abs(levels - a[p, g]) >= 10]
            a[p, g + 8] = far[np.random.randint(len(far))]
    return np.exp2(a.ravel()).repeat(32)


def f64(x):
    return np.asarray(x).astype(np.float64)


def striped(idx):
    return np.tile(idx.reshape(-1, 16).T, (8, 1)).astype(np.uint16)


def unstriped(offs):
    return offs[:16].T.reshape(-1).astype(np.int64)


E2M1 = np.array([0.0, 0.5, 1.0, 1.5, 2.0, 3.0, 4.0, 6.0, -0.0, -0.5, -1.0, -1.5, -2.0, -3.0, -4.0, -6.0])


def pack_weight(w, fmt):
    k, n = w.shape
    w = f64(np.asarray(w, np.float32).astype(ml_dtypes.bfloat16)).reshape(k // 32, 32, n)
    amax = np.abs(w).max(1)
    if fmt == "e4m3":
        byte = np.frexp(amax)[1] - 1 + 127 - 7
    else:
        mant, ex = np.frexp(amax / 6.0)
        byte = np.where(mant > 0.5, ex, ex - 1) + 127
    byte = np.clip(np.where(amax > 0, byte, 1), 1, 254)
    scaled = (w * np.exp2(127.0 - byte)[:, None, :]).reshape(k, n).astype(np.float32)
    by_word = np.ascontiguousarray(scaled.reshape(k // 512, 128, 4, n).transpose(0, 1, 3, 2))
    if fmt == "e4m3":
        words = by_word.astype(ml_dtypes.float8_e4m3fn).view(np.uint8)
    else:
        c = by_word.astype(ml_dtypes.float4_e2m1fn).view(np.uint8) & 0xF
        words = (c[..., 0::2] | (c[..., 1::2] << 4)).reshape(k // 512, 128, 2 * n)
    return np.ascontiguousarray(words), np.ascontiguousarray(byte.astype(np.uint8).reshape(k // 512, 16, n))


def unpack_weight(words, scales, fmt):
    g, _, n = scales.shape
    words = np.ascontiguousarray(words).reshape(g, 128, n, -1)
    if fmt == "e4m3":
        vals = words.view(ml_dtypes.float8_e4m3fn).astype(np.float64)
    else:
        nib = np.empty((g, 128, n, 4), np.uint8)
        nib[..., 0::2] = words & 0xF
        nib[..., 1::2] = words >> 4
        vals = E2M1[nib]
    vals = vals * np.repeat(np.exp2(scales.astype(np.float64) - 127.0), 8, axis=1)[..., None]
    return vals.transpose(0, 1, 3, 2).reshape(g * 512, n)


def d_relu2(v):
    return 2.0 * np.maximum(v, 0.0)


K, T, E, C, H, N = 512, 768, 2, 256, 1024, 2048


def by_expert(wq, xq):
    return np.concatenate([wq[e].T @ xq[:, e * C:(e + 1) * C] for e in range(E)], axis=1)


def setup_inputs():
    n = np.random.standard_normal
    s = mx_kscale(N)[:, None]
    u = mx_kscale(H)
    w2 = [pack_weight(m, "e2m1") for m in n((E, N, H)) / np.sqrt(N) / s[None] * u[None, None, :]]
    w1 = [pack_weight(m, "e2m1") for m in n((E, H, K)) / np.sqrt(H) / u[None, :, None]]
    return {
        "dyT": (n((N, T)) * s).astype(np.float32),
        "a": n((H, E * C)).astype(np.float32),
        "w2_words": np.stack([m[0] for m in w2]),
        "w2_scales": np.stack([m[1] for m in w2]),
        "w1_words": np.stack([m[0] for m in w1]),
        "w1_scales": np.stack([m[1] for m in w1]),
        "gate": np.tile(np.random.uniform(0.2, 1.0, E * C), (N, 1)).astype(np.float32),
        "offs": striped(np.random.permutation(T)[:E * C]),
    }


def reference(dyT, a, w2_words, w2_scales, w1_words, w1_scales, gate, offs):
    idx = unstriped(offs)
    w2 = np.stack([unpack_weight(w2_words[e], w2_scales[e], "e2m1") for e in range(E)])
    w1 = np.stack([unpack_weight(w1_words[e], w1_scales[e], "e2m1") for e in range(E)])
    gq = mxq(f64(gate) * f64(dyT)[:, idx], 0, "e4m3")
    dh = by_expert(w2, gq)
    da = dh * d_relu2(f64(a))
    dx = by_expert(w1, mxq(da, 0, "e4m3"))
    out = np.zeros((K, T))
    out[:, idx] = dx
    return out

@@ -1,0 +1,208 @@
+import concourse.mybir as mybir
+from concourse.masks import make_identity
+
+K, T, E, C, H, N = 512, 768, 2, 256, 1024, 2048
+P = 128
+S = E * C
+NS = N // 512
+QS = H // 512
+KB = K // P
+UNITS = S // P
+
+FLOPS = 2 * N * H * S + 2 * H * K * S
+BYTES = 4 * (N * T + H * S + S + K * T) + E * (N * H // 2 + H * K // 2) + E * (N * H + H * K) // 32 + 128 * 32 * 2
+
+F32 = mybir.dt.float32
+BF16 = mybir.dt.bfloat16
+I32 = mybir.dt.int32
+U32 = mybir.dt.uint32
+U16 = mybir.dt.uint16
+U8 = mybir.dt.uint8
+FP8X4 = mybir.dt.float8_e4m3fn_x4
+FP4X4 = mybir.dt.float4_e2m1fn_x4
+MULT = mybir.AluOpType.mult
+MAX = mybir.AluOpType.max
+COPY = mybir.ActivationFunctionType.Copy
+
+GROUPS = {0: [(0, 512)], 1: [(0, 512)], 2: [(0, 512)], 3: [(0, 256), (256, 512)]}
+
+
+def tile_moe_bdx_mlp_relu2_kernel(tc, dyT, a, w2_words, w2_scales, w1_words, w1_scales, gate, offs, out):
+    nc = tc.nc
+    with (
+        tc.tile_pool(name="held", bufs=1) as held,
+        tc.tile_pool(name="graw", bufs=2) as graw_pool,
+        tc.tile_pool(name="gbf", bufs=2) as gbf_pool,
+        tc.tile_pool(name="stage", bufs=3) as stage,
+        tc.psum_pool(name="psdh", bufs=5) as psdh,
+        tc.psum_pool(name="pst", bufs=2) as pst,
+        tc.psum_pool(name="psdx", bufs=1) as psdx,
+    ):
+        offsets = held.tile([P, S // 16], U16, name="offsets")
+        nc.sync.dma_start(offsets[:], offs)
+        gate_sb = held.tile([P, S], F32, name="gate_sb")
+        nc.sync.dma_start(gate_sb[:], gate[0:P, :])
+
+        dy_rows = dyT.rearrange("(s p t) w -> s t p w", p=P, t=4)
+        dy = {}
+
+        def load_dy(s):
+            for t in range(4):
+                tile = held.tile([P, T], F32, name=f"dy{s}{t}")
+                nc.sync.dma_start(tile[:], dy_rows[s, t])
+                dy[s, t] = tile
+
+        w2w = held.tile([P, E, NS, 2 * H], U8, name="w2w", align_bytes=64)
+        w2s = held.tile([P, E * NS, H], U8, name="w2s", align_bytes=64)
+        w1w = held.tile([P, E, QS, 2 * K], U8, name="w1w", align_bytes=64)
+        w1s = held.tile([P, E * QS, K], U8, name="w1s", align_bytes=64)
+        a_sb = held.tile([P, QS, 4, S], F32, name="a_sb")
+
+        def load_w2(e, s0):
+            nc.sync.dma_start(
+                w2w[:, e, s0 : s0 + 2, :].bitcast(I32),
+                w2_words[e, s0 : s0 + 2].rearrange("s p b -> p s b").bitcast(I32),
+            )
+
+        nc.vector.memset(w2s[:].rearrange("p x i -> p (x i)").bitcast(I32), 0)
+        nc.vector.memset(w1s[:].rearrange("p x i -> p (x i)").bitcast(I32), 0)
+        windows = []
+        for kb in range(KB):
+            win = held.tile([P, T], F32, name=f"win{kb}")
+            nc.vector.memset(win[:], 0.0)
+            windows.append(win)
+        ident = held.tile([P, P], F32, name="ident")
+        make_identity(nc, ident[:])
+
+        load_dy(0)
+        load_dy(1)
+        for q in range(4):
+            nc.sync.dma_start(
+                w2s[32 * q : 32 * q + 4, :, :].bitcast(I32),
+                w2_scales[:, :, 4 * q : 4 * q + 4, :].rearrange("e s f i -> f (e s) i").bitcast(I32),
+            )
+        load_w2(0, 0)
+        load_dy(2)
+        load_w2(0, 2)
+        load_dy(3)
+        for q in range(QS):
+            nc.sync.dma_start(a_sb[:, q], a[512 * q : 512 * (q + 1), :].rearrange("(p t) n -> p t n", t=4))
+        nc.sync.dma_start(w1w[:].rearrange("p e q b -> p (e q) b").bitcast(I32), w1_words.rearrange("e q p b -> p (e q) b").bitcast(I32))
+        for q in range(4):
+            nc.sync.dma_start(
+                w1s[32 * q : 32 * q + 4, :, :].bitcast(I32),
+                w1_scales[:, :, 4 * q : 4 * q + 4, :].rearrange("e s f i -> f (e s) i").bitcast(I32),
+            )
+        load_w2(1, 0)
+        load_w2(1, 2)
+
+        g_codes = held.tile([P, NS, S], U32, name="g_codes", align_bytes=64)
+        g_scales = held.tile([P, NS, S], U8, name="g_scales", align_bytes=64)
+
+        def gather(s, c0, c1):
+            raw = graw_pool.tile([P, 4, c1 - c0], F32, name=f"raw{c1 - c0}")
+            for t in range(4):
+                nc.vector.tensor_tensor(raw[:, t, :], dy[s, t][:].indirect(offsets[:, c0 // 16 : c1 // 16]), gate_sb[:, c0:c1], MULT)
+            bf = gbf_pool.tile([P, c1 - c0, 4], BF16, name=f"bf{c1 - c0}", align_bytes=64)
+            for h0 in range(0, c1 - c0, 256):
+                nc.scalar.copy(bf[:, h0 : h0 + 256, :], raw[:, :, h0 : h0 + 256].rearrange("p t n -> p n t"))
+            return bf
+
+        def quant(s, c0, c1, bf):
+            nc.vector.quantize_mx(g_codes[:, s, c0:c1].bitcast(FP8X4), g_scales[:, s, c0:c1], bf[:].rearrange("p n t -> p (n t)"))
+
+        dh = {}
+
+        def dh_pass(u, s):
+            e = u // 2
+            cols = slice(P * u, P * (u + 1))
+            for q in range(QS):
+                if s == 0:
+                    dh[u, q] = psdh.tile([P, 512], F32, name="dh")
+                nc.tensor.matmul_mx(
+                    dh[u, q][:],
+                    lhsT=g_codes[:, s, cols].bitcast(FP8X4),
+                    lhsT_scale=g_scales[:, s, cols],
+                    rhs=w2w[:, e, s, 1024 * q : 1024 * (q + 1)].bitcast(FP4X4),
+                    rhs_scale=w2s[:, NS * e + s, 512 * q : 512 * (q + 1)],
+                    start=(s == 0),
+                    stop=(s == NS - 1),
+                )
+
+        def da_unit(u):
+            cols = slice(P * u, P * (u + 1))
+            da = stage.tile([P, QS, 512], BF16, name="da", align_bytes=64)
+            for q in range(QS):
+                dhs = stage.tile([P, 4, P], F32, name="dhs")
+                nc.scalar.activation(dhs[:], dh[u, q][:].rearrange("p (m t) -> p t m", t=4), COPY, scale=2.0)
+                tp = pst.tile([P, 4, P], F32, name="tp")
+                for t in range(4):
+                    nc.tensor.transpose(tp[:, t, :], dhs[:, t, :], ident[:])
+                nc.vector.scalar_tensor_tensor(
+                    da[:, q, :].rearrange("p (n t) -> p n t", t=4),
+                    a_sb[:, q, :, cols].rearrange("p t n -> p n t"),
+                    0.0,
+                    tp[:].rearrange("p t n -> p n t"),
+                    MAX,
+                    MULT,
+                )
+            return da
+
+        def dx_unit(u, da):
+            e = u // 2
+            codes = stage.tile([P, QS, P], U32, name="da_codes", align_bytes=64)
+            scales = stage.tile([P, QS, P], U8, name="da_scales", align_bytes=64)
+            nc.vector.quantize_mx(
+                codes[:].rearrange("p q n -> p (q n)").bitcast(FP8X4),
+                scales[:].rearrange("p q n -> p (q n)"),
+                da[:].rearrange("p q x -> p (q x)"),
+            )
+            ps = psdx.tile([P, KB, P], F32, name="dx")
+            for kb in range(KB):
+                for q in range(QS):
+                    nc.tensor.matmul_mx(
+                        ps[:, kb, :],
+                        lhsT=w1w[:, e, q, 256 * kb : 256 * (kb + 1)].bitcast(FP4X4),
+                        lhsT_scale=w1s[:, QS * e + q, P * kb : P * (kb + 1)],
+                        rhs=codes[:, q, :].bitcast(FP8X4),
+                        rhs_scale=scales[:, q, :],
+                        start=(q == 0),
+                        stop=(q == QS - 1),
+                    )
+            dxs = stage.tile([P, KB, P], F32, name="dxs")
+            nc.scalar.copy(dxs[:], ps[:])
+            return dxs
+
+        def scatter(u, dxs):
+            for kb in range(KB):
+                nc.vector.tensor_copy(windows[kb][:].indirect(offsets[:, 8 * u : 8 * (u + 1)]), dxs[:, kb, :])
+
+        for s in range(3):
+            bf = gather(s, 0, S)
+            quant(s, 0, S, bf)
+            dh_pass(0, s)
+            dh_pass(1, s)
+        bf0 = gather(3, 0, C)
+        quant(3, 0, C, bf0)
+        dh_pass(0, 3)
+        dh_pass(1, 3)
+        bf1 = gather(3, C, S)
+        quant(3, C, S, bf1)
+        da0 = da_unit(0)
+        dx0 = dx_unit(0, da0)
+        da1 = da_unit(1)
+        dx1 = dx_unit(1, da1)
+        for s in range(NS):
+            dh_pass(2, s)
+        for s in range(NS):
+            dh_pass(3, s)
+        scatter(0, dx0)
+        da2 = da_unit(2)
+        scatter(1, dx1)
+        dx2 = dx_unit(2, da2)
+        da3 = da_unit(3)
+        dx3 = dx_unit(3, da3)
+        scatter(2, dx2)
+        scatter(3, dx3)
+        for kb in range(KB):
+            nc.sync.dma_start(out[P * kb : P * (kb + 1), :], windows[kb][:])

@@ -24,8 +24,6 @@ MULT = mybir.AluOpType.mult
 MAX = mybir.AluOpType.max
 COPY = mybir.ActivationFunctionType.Copy
 
-GROUPS = {0: [(0, 512)], 1: [(0, 512)], 2: [(0, 512)], 3: [(0, 256), (256, 512)]}
-
 
 def tile_moe_bdx_mlp_relu2_kernel(tc, dyT, a, w2_words, w2_scales, w1_words, w1_scales, gate, offs, out):
     nc = tc.nc
@@ -69,10 +67,11 @@ def tile_moe_bdx_mlp_relu2_kernel(tc, dyT, a, w2_words, w2_scales, w1_words, w1_
         windows = []
         for kb in range(KB):
             win = held.tile([P, T], F32, name=f"win{kb}")
-            nc.vector.memset(win[:], 0.0)
             windows.append(win)
         ident = held.tile([P, P], F32, name="ident")
         make_identity(nc, ident[:])
+        for win in windows:
+            nc.scalar.activation(win[:], ident[:, 0:1].to_broadcast([P, T]), COPY, scale=0.0)
 
         load_dy(0)
         load_dy(1)
@@ -85,6 +84,8 @@ def tile_moe_bdx_mlp_relu2_kernel(tc, dyT, a, w2_words, w2_scales, w1_words, w1_
         load_dy(2)
         load_w2(0, 2)
         load_dy(3)
+        load_w2(1, 0)
+        load_w2(1, 2)
         for q in range(QS):
             nc.sync.dma_start(a_sb[:, q], a[512 * q : 512 * (q + 1), :].rearrange("(p t) n -> p t n", t=4))
         nc.sync.dma_start(w1w[:].rearrange("p e q b -> p (e q) b").bitcast(I32), w1_words.rearrange("e q p b -> p (e q) b").bitcast(I32))
@@ -93,8 +94,6 @@ def tile_moe_bdx_mlp_relu2_kernel(tc, dyT, a, w2_words, w2_scales, w1_words, w1_
                 w1s[32 * q : 32 * q + 4, :, :].bitcast(I32),
                 w1_scales[:, :, 4 * q : 4 * q + 4, :].rearrange("e s f i -> f (e s) i").bitcast(I32),
             )
-        load_w2(1, 0)
-        load_w2(1, 2)
 
         g_codes = held.tile([P, NS, S], U32, name="g_codes", align_bytes=64)
         g_scales = held.tile([P, NS, S], U8, name="g_scales", align_bytes=64)

import concourse.mybir as mybir
from concourse.masks import make_identity

K, T, E, C, H, N = 512, 768, 2, 256, 1024, 2048
P = 128
S = E * C
NS = N // 512
QS = H // 512
KB = K // P
UNITS = S // P

FLOPS = 2 * N * H * S + 2 * H * K * S
BYTES = 4 * (N * T + H * S + S + K * T) + E * (N * H // 2 + H * K // 2) + E * (N * H + H * K) // 32 + 128 * 32 * 2

F32 = mybir.dt.float32
BF16 = mybir.dt.bfloat16
I32 = mybir.dt.int32
U32 = mybir.dt.uint32
U16 = mybir.dt.uint16
U8 = mybir.dt.uint8
FP8X4 = mybir.dt.float8_e4m3fn_x4
FP4X4 = mybir.dt.float4_e2m1fn_x4
MULT = mybir.AluOpType.mult
MAX = mybir.AluOpType.max
COPY = mybir.ActivationFunctionType.Copy


def tile_moe_bdx_mlp_relu2_kernel(tc, dyT, a, w2_words, w2_scales, w1_words, w1_scales, gate, offs, out):
    nc = tc.nc
    with (
        tc.tile_pool(name="held", bufs=1) as held,
        tc.tile_pool(name="graw", bufs=2) as graw_pool,
        tc.tile_pool(name="gbf", bufs=2) as gbf_pool,
        tc.tile_pool(name="stage", bufs=3) as stage,
        tc.psum_pool(name="psdh", bufs=5) as psdh,
        tc.psum_pool(name="pst", bufs=2) as pst,
        tc.psum_pool(name="psdx", bufs=1) as psdx,
    ):
        offsets = held.tile([P, S // 16], U16, name="offsets")
        nc.sync.dma_start(offsets[:], offs)
        gate_sb = held.tile([P, S], F32, name="gate_sb")
        nc.sync.dma_start(gate_sb[:], gate[0:P, :])

        dy_rows = dyT.rearrange("(s p t) w -> s t p w", p=P, t=4)
        dy = {}

        def load_dy(s):
            for t in range(4):
                tile = held.tile([P, T], F32, name=f"dy{s}{t}")
                nc.sync.dma_start(tile[:], dy_rows[s, t])
                dy[s, t] = tile

        w2w = held.tile([P, E, NS, 2 * H], U8, name="w2w", align_bytes=64)
        w2s = held.tile([P, E * NS, H], U8, name="w2s", align_bytes=64)
        w1w = held.tile([P, E, QS, 2 * K], U8, name="w1w", align_bytes=64)
        w1s = held.tile([P, E * QS, K], U8, name="w1s", align_bytes=64)
        a_sb = held.tile([P, QS, 4, S], F32, name="a_sb")

        def load_w2(e, s0):
            nc.sync.dma_start(
                w2w[:, e, s0 : s0 + 2, :].bitcast(I32),
                w2_words[e, s0 : s0 + 2].rearrange("s p b -> p s b").bitcast(I32),
            )

        nc.vector.memset(w2s[:].rearrange("p x i -> p (x i)").bitcast(I32), 0)
        nc.vector.memset(w1s[:].rearrange("p x i -> p (x i)").bitcast(I32), 0)
        windows = []
        for kb in range(KB):
            win = held.tile([P, T], F32, name=f"win{kb}")
            windows.append(win)
        ident = held.tile([P, P], F32, name="ident")
        make_identity(nc, ident[:])
        for win in windows:
            nc.scalar.activation(win[:], ident[:, 0:1].to_broadcast([P, T]), COPY, scale=0.0)

        load_dy(0)
        load_dy(1)
        for q in range(4):
            nc.sync.dma_start(
                w2s[32 * q : 32 * q + 4, :, :].bitcast(I32),
                w2_scales[:, :, 4 * q : 4 * q + 4, :].rearrange("e s f i -> f (e s) i").bitcast(I32),
            )
        load_w2(0, 0)
        load_dy(2)
        load_w2(0, 2)
        load_dy(3)
        load_w2(1, 0)
        load_w2(1, 2)
        for q in range(QS):
            nc.sync.dma_start(a_sb[:, q], a[512 * q : 512 * (q + 1), :].rearrange("(p t) n -> p t n", t=4))
        nc.sync.dma_start(w1w[:].rearrange("p e q b -> p (e q) b").bitcast(I32), w1_words.rearrange("e q p b -> p (e q) b").bitcast(I32))
        for q in range(4):
            nc.sync.dma_start(
                w1s[32 * q : 32 * q + 4, :, :].bitcast(I32),
                w1_scales[:, :, 4 * q : 4 * q + 4, :].rearrange("e s f i -> f (e s) i").bitcast(I32),
            )

        g_codes = held.tile([P, NS, S], U32, name="g_codes", align_bytes=64)
        g_scales = held.tile([P, NS, S], U8, name="g_scales", align_bytes=64)

        def gather(s, c0, c1):
            raw = graw_pool.tile([P, 4, c1 - c0], F32, name=f"raw{c1 - c0}")
            for t in range(4):
                nc.vector.tensor_tensor(raw[:, t, :], dy[s, t][:].indirect(offsets[:, c0 // 16 : c1 // 16]), gate_sb[:, c0:c1], MULT)
            bf = gbf_pool.tile([P, c1 - c0, 4], BF16, name=f"bf{c1 - c0}", align_bytes=64)
            for h0 in range(0, c1 - c0, 256):
                nc.scalar.copy(bf[:, h0 : h0 + 256, :], raw[:, :, h0 : h0 + 256].rearrange("p t n -> p n t"))
            return bf

        def quant(s, c0, c1, bf):
            nc.vector.quantize_mx(g_codes[:, s, c0:c1].bitcast(FP8X4), g_scales[:, s, c0:c1], bf[:].rearrange("p n t -> p (n t)"))

        dh = {}

        def dh_pass(u, s):
            e = u // 2
            cols = slice(P * u, P * (u + 1))
            for q in range(QS):
                if s == 0:
                    dh[u, q] = psdh.tile([P, 512], F32, name="dh")
                nc.tensor.matmul_mx(
                    dh[u, q][:],
                    lhsT=g_codes[:, s, cols].bitcast(FP8X4),
                    lhsT_scale=g_scales[:, s, cols],
                    rhs=w2w[:, e, s, 1024 * q : 1024 * (q + 1)].bitcast(FP4X4),
                    rhs_scale=w2s[:, NS * e + s, 512 * q : 512 * (q + 1)],
                    start=(s == 0),
                    stop=(s == NS - 1),
                )

        def da_unit(u):
            cols = slice(P * u, P * (u + 1))
            da = stage.tile([P, QS, 512], BF16, name="da", align_bytes=64)
            for q in range(QS):
                dhs = stage.tile([P, 4, P], F32, name="dhs")
                nc.scalar.activation(dhs[:], dh[u, q][:].rearrange("p (m t) -> p t m", t=4), COPY, scale=2.0)
                tp = pst.tile([P, 4, P], F32, name="tp")
                for t in range(4):
                    nc.tensor.transpose(tp[:, t, :], dhs[:, t, :], ident[:])
                nc.vector.scalar_tensor_tensor(
                    da[:, q, :].rearrange("p (n t) -> p n t", t=4),
                    a_sb[:, q, :, cols].rearrange("p t n -> p n t"),
                    0.0,
                    tp[:].rearrange("p t n -> p n t"),
                    MAX,
                    MULT,
                )
            return da

        def dx_unit(u, da):
            e = u // 2
            codes = stage.tile([P, QS, P], U32, name="da_codes", align_bytes=64)
            scales = stage.tile([P, QS, P], U8, name="da_scales", align_bytes=64)
            nc.vector.quantize_mx(
                codes[:].rearrange("p q n -> p (q n)").bitcast(FP8X4),
                scales[:].rearrange("p q n -> p (q n)"),
                da[:].rearrange("p q x -> p (q x)"),
            )
            ps = psdx.tile([P, KB, P], F32, name="dx")
            for kb in range(KB):
                for q in range(QS):
                    nc.tensor.matmul_mx(
                        ps[:, kb, :],
                        lhsT=w1w[:, e, q, 256 * kb : 256 * (kb + 1)].bitcast(FP4X4),
                        lhsT_scale=w1s[:, QS * e + q, P * kb : P * (kb + 1)],
                        rhs=codes[:, q, :].bitcast(FP8X4),
                        rhs_scale=scales[:, q, :],
                        start=(q == 0),
                        stop=(q == QS - 1),
                    )
            dxs = stage.tile([P, KB, P], F32, name="dxs")
            nc.scalar.copy(dxs[:], ps[:])
            return dxs

        def scatter(u, dxs):
            for kb in range(KB):
                nc.vector.tensor_copy(windows[kb][:].indirect(offsets[:, 8 * u : 8 * (u + 1)]), dxs[:, kb, :])

        for s in range(3):
            bf = gather(s, 0, S)
            quant(s, 0, S, bf)
            dh_pass(0, s)
            dh_pass(1, s)
        bf0 = gather(3, 0, C)
        quant(3, 0, C, bf0)
        dh_pass(0, 3)
        dh_pass(1, 3)
        bf1 = gather(3, C, S)
        quant(3, C, S, bf1)
        da0 = da_unit(0)
        dx0 = dx_unit(0, da0)
        da1 = da_unit(1)
        dx1 = dx_unit(1, da1)
        for s in range(NS):
            dh_pass(2, s)
        for s in range(NS):
            dh_pass(3, s)
        scatter(0, dx0)
        da2 = da_unit(2)
        scatter(1, dx1)
        dx2 = dx_unit(2, da2)
        da3 = da_unit(3)
        dx3 = dx_unit(3, da3)
        scatter(2, dx2)
        scatter(3, dx3)
        for kb in range(KB):
            nc.sync.dma_start(out[P * kb : P * (kb + 1), :], windows[kb][:])
